import numpy as np
import ml_dtypes


def mxq(x, axis, fmt="e4m3"):
    dtype, down = {"e4m3": (ml_dtypes.float8_e4m3fn, 7), "e5m2": (ml_dtypes.float8_e5m2, 14)}[fmt]
    v = np.moveaxis(np.asarray(x, np.float32).astype(ml_dtypes.bfloat16).astype(np.float64), axis, -1)
    blocks = v.reshape(v.shape[:-1] + (-1, 32))
    amax = np.abs(blocks).max(-1, keepdims=True)
    byte = np.maximum(np.where(amax > 0, np.frexp(amax)[1] - 1 + 127, 0) - down, 1)
    scale = np.exp2(byte - 127.0)
    codes = (blocks / scale).astype(np.float32).astype(dtype).astype(np.float64)
    return np.moveaxis((codes * scale).reshape(v.shape), -1, axis)


WIDE = False


def mx_kscale(k):
    if not WIDE:
        return np.ones(k)
    levels = np.array([10, -10, 5, -5, 0])
    if k % 512:
        return np.exp2(np.random.permutation(np.resize(levels, k // 32))).repeat(32)
    a = np.empty((k // 512, 16))
    for p in range(k // 512):
        a[p, :8] = np.random.permutation(np.resize(levels, 8))
        for g in range(8):
            far = levels[np.abs(levels - a[p, g]) >= 10]
            a[p, g + 8] = far[np.random.randint(len(far))]
    return np.exp2(a.ravel()).repeat(32)


def f64(x):
    return np.asarray(x).astype(np.float64)


def striped(idx):
    return np.tile(idx.reshape(-1, 16).T, (8, 1)).astype(np.uint16)


def unstriped(offs):
    return offs[:16].T.reshape(-1).astype(np.int64)


def gelu(v):
    return 0.5 * v * (1.0 + np.tanh(np.sqrt(2.0 / np.pi) * (v + 0.044715 * v**3)))


K, T, E, C, H, N = 1024, 1024, 8, 128, 512, 128


def by_expert(wq, xq):
    return np.concatenate([wq[e].T @ xq[:, e * C:(e + 1) * C] for e in range(E)], axis=1)


def setup_inputs():
    n = np.random.standard_normal
    s = mx_kscale(K)[:, None]
    u = mx_kscale(H)
    return {
        "xT": (n((K, T)) * s).astype(np.float32),
        "w1": (n((E, K, H)) / np.sqrt(K) / s[None]).astype(np.float32),
        "w3": (n((E, K, H)) / np.sqrt(K) / s[None] * u[None, None, :]).astype(np.float32),
        "w2": (n((E, H, N)) / np.sqrt(H) / u[None, :, None]).astype(np.float32),
        "gate": np.tile(np.random.uniform(0.2, 1.0, E * C), (N, 1)).astype(np.float32),
        "offs": striped(np.random.permutation(T)[:E * C]),
    }


def reference(xT, w1, w3, w2, gate, offs):
    idx = unstriped(offs)
    xq = mxq(f64(xT)[:, idx], 0, "e4m3")
    h = gelu(by_expert(mxq(f64(w1), 1, "e4m3"), xq))
    h = h * by_expert(mxq(f64(w3), 1, "e4m3"), xq)
    y = by_expert(mxq(f64(w2), 1, "e4m3"), mxq(h, 0, "e4m3"))
    out = np.zeros((N, T))
    out[:, idx] = f64(gate) * y
    return out

@@ -1,0 +1,208 @@
+from contextlib import ExitStack
+
+import concourse.mybir as mybir
+
+K, T, E, C, H, N = 1024, 1024, 8, 128, 512, 128
+FLOPS = 2 * E * C * (2 * K * H + H * N)
+
+F32 = mybir.dt.float32
+BF16 = mybir.dt.bfloat16
+U32 = mybir.dt.uint32
+U16 = mybir.dt.uint16
+U8 = mybir.dt.uint8
+FP8X4 = mybir.dt.float8_e4m3fn_x4
+GELU = mybir.ActivationFunctionType.Gelu_apprx_tanh
+MULT = mybir.AluOpType.mult
+
+P = 128
+PACK = 4
+K_PASS = P * PACK
+PASSES = K // K_PASS
+CHUNK = 2048
+HALF = 512
+
+
+def tile_routed_moe_kernel(tc, xT, w1, w3, w2, gate, offs, out):
+    nc = tc.nc
+    with ExitStack() as ctx:
+        held = ctx.enter_context(tc.tile_pool(name="held", bufs=1))
+        stream = ctx.enter_context(tc.tile_pool(name="stream", bufs=8))
+        grouped = ctx.enter_context(tc.tile_pool(name="grouped", bufs=2))
+        quant = ctx.enter_context(tc.tile_pool(name="quant", bufs=10))
+        small = ctx.enter_context(tc.tile_pool(name="small", bufs=2))
+        order = ctx.enter_context(tc.tile_pool(name="order", bufs=1))
+        psum = ctx.enter_context(tc.psum_pool(name="psum", bufs=2))
+
+        offsets = held.tile([P, E * C // 16], U16, name="offsets")
+        nc.sync.dma_start(offsets[:], offs)
+
+        warm_in = held.tile([P, 1], F32, name="warm_in")
+        warm_out = held.tile([P, 1], F32, name="warm_out")
+        nc.vector.memset(warm_in[:], 0.0)
+        nc.scalar.activation(warm_out[:], warm_in[:], GELU)
+
+        def copy_on(engine, dst, src):
+            if engine == "V":
+                nc.vector.tensor_copy(out=dst, in_=src)
+            else:
+                nc.scalar.copy(out=dst, in_=src)
+
+        x_planes = xT.rearrange("(g p u e) n -> g u p (e n)", p=P, u=2, e=2)
+        pairs = {}
+        for g in range(PASSES):
+            for u in range(2):
+                raw = stream.tile([P, CHUNK], F32, tag="raw", name="xraw%d%d" % (g, u))
+                nc.sync.dma_start(raw[:], x_planes[g, u])
+                pair = held.tile([P, 2 * T], BF16, name="pair%d%d" % (g, u))
+                copy_on(
+                    "S",
+                    pair[:].rearrange("p (n e) -> p n e", e=2),
+                    raw[:].rearrange("p (e n) -> p n e", e=2),
+                )
+                pairs[(g, u)] = pair
+
+        gate_sb = held.tile([P, E * C], F32, name="gate_sb")
+        nc.sync.dma_start(gate_sb[:], gate)
+
+        x_codes = []
+        x_scales = []
+        for g in range(PASSES):
+            xg = held.tile([P, PACK * E * C], BF16, name="xg%d" % g, align_bytes=64)
+            xg_words = xg[:].bitcast(U32).rearrange("p (s u) -> p s u", u=2)
+            for u in range(2):
+                for h in range(E * C // HALF):
+                    nc.vector.tensor_copy(
+                        out=xg_words[:, h * HALF : (h + 1) * HALF, u],
+                        in_=pairs[(g, u)][:].bitcast(U32).indirect(offsets[:, h * HALF // 16 : (h + 1) * HALF // 16]),
+                    )
+            xc = held.tile([P, E * C], U32, name="xc%d" % g, align_bytes=64)
+            xs = held.tile([P, E * C], U8, name="xs%d" % g, align_bytes=64)
+            for h in range(E * C // HALF):
+                nc.vector.quantize_mx(
+                    out=xc[:, h * HALF : (h + 1) * HALF].bitcast(FP8X4),
+                    scales=xs[:, h * HALF : (h + 1) * HALF],
+                    in_=xg[:, h * HALF * PACK : (h + 1) * HALF * PACK],
+                )
+            x_codes.append(xc)
+            x_scales.append(xs)
+
+        w2_rows = w2.rearrange("e (p j) n -> p e (j n)", p=P, j=PACK)
+        w2_codes = []
+        w2_scales = []
+        for half in range(2):
+            raw = stream.tile([P, CHUNK], F32, tag="raw", name="w2raw%d" % half)
+            nc.sync.dma_start(raw[:].rearrange("p (e f) -> p e f", e=4), w2_rows[:, 4 * half : 4 * half + 4, :])
+            wi = grouped.tile([P, CHUNK], BF16, tag="wi", name="w2i%d" % half, align_bytes=64)
+            copy_on(
+                "S",
+                wi[:].rearrange("p (e c i j) -> p e c j i", e=4, i=4, j=PACK),
+                raw[:].rearrange("p (e j c i) -> p e c j i", e=4, i=4, j=PACK),
+            )
+            wc = held.tile([P, CHUNK // PACK], U32, name="w2c%d" % half, align_bytes=64)
+            ws = held.tile([P, CHUNK // PACK], U8, name="w2s%d" % half, align_bytes=64)
+            nc.vector.quantize_mx(out=wc[:].bitcast(FP8X4), scales=ws[:], in_=wi[:])
+            w2_codes.append(wc)
+            w2_scales.append(ws)
+
+        window = held.tile([P, T], F32, name="window")
+
+        def load_chunk(w, e, g, label):
+            raw = stream.tile([P, CHUNK], F32, tag="raw", name="raw_%s" % label)
+            nc.sync.dma_start(raw[:], w[e].rearrange("(g p j) c -> g p (j c)", p=P, j=PACK)[g])
+            return raw
+
+        def interleave(raw, engine, pool, tag, label):
+            wi = pool.tile([P, CHUNK], BF16, tag=tag, name="wi_%s" % label, align_bytes=64)
+            copy_on(
+                engine,
+                wi[:].rearrange("p (t m j) -> p m j t", t=4, j=PACK),
+                raw[:].rearrange("p (j m t) -> p m j t", t=4, j=PACK),
+            )
+            return wi
+
+        def quantise(wi, label):
+            wc = quant.tile([P, H], U32, tag="wc", name="wc_%s" % label, align_bytes=64)
+            ws = quant.tile([P, H], U8, tag="ws", name="ws_%s" % label, align_bytes=64)
+            nc.vector.quantize_mx(out=wc[:].bitcast(FP8X4), scales=ws[:], in_=wi[:])
+            return wc, ws
+
+        def first_layer(acc, codes, e):
+            slots = slice(e * C, (e + 1) * C)
+            for t in range(4):
+                cols = slice(t * P, (t + 1) * P)
+                for g in range(PASSES):
+                    wc, ws = codes[g]
+                    nc.tensor.matmul_mx(
+                        out=acc[:, t, :],
+                        lhsT=wc[:, cols].bitcast(FP8X4),
+                        lhsT_scale=ws[:, cols],
+                        rhs=x_codes[g][:, slots].bitcast(FP8X4),
+                        rhs_scale=x_scales[g][:, slots],
+                        start=(g == 0),
+                        stop=(g == PASSES - 1),
+                    )
+
+        st = {}
+        for i in range(E + 1):
+            e = i
+            d = i - 1
+            if i < E:
+                raws = [
+                    load_chunk(w1, e, 0, "a%d0" % e),
+                    load_chunk(w1, e, 1, "a%d1" % e),
+                    load_chunk(w3, e, 0, "b%d0" % e),
+                    load_chunk(w3, e, 1, "b%d1" % e),
+                ]
+                wi_a0 = interleave(raws[0], "V", order, "ta", "a%d0" % e)
+            if i > 0:
+                cb1 = quantise(st["wi_b1"], "b%d1" % d)
+                acc_b = psum.tile([P, 4, C], F32, tag="acc_b", name="acc_b%d" % d)
+                first_layer(acc_b, [st["cb0"], cb1], d)
+            if i < E:
+                ca0 = quantise(wi_a0, "a%d0" % e)
+            if i > 0:
+                hq = order.tile([P, PACK * C], BF16, tag="ta", name="hq%d" % d, align_bytes=64)
+                nc.vector.tensor_tensor(
+                    out=hq[:].rearrange("p (c t) -> p c t", t=4),
+                    in0=acc_b[:].rearrange("p t c -> p c t"),
+                    in1=st["ga"][:].rearrange("p (c t) -> p c t", t=4),
+                    op=MULT,
+                )
+            if i < E:
+                wi_a1 = interleave(raws[1], "S", order, "tb", "a%d1" % e)
+                ca1 = quantise(wi_a1, "a%d1" % e)
+                acc_a = psum.tile([P, 4, C], F32, tag="acc_a", name="acc_a%d" % e)
+                first_layer(acc_a, [ca0, ca1], e)
+            if i > 0:
+                hc = order.tile([P, C], U32, tag="tb", name="hc%d" % d, align_bytes=64)
+                hs = small.tile([P, C], U8, tag="hs", name="hs%d" % d, align_bytes=64)
+                nc.vector.quantize_mx(out=hc[:].bitcast(FP8X4), scales=hs[:], in_=hq[:])
+                acc_y = psum.tile([P, C], F32, tag="acc_y", name="acc_y%d" % d)
+                cols = slice((d % 4) * N, (d % 4 + 1) * N)
+                nc.tensor.matmul_mx(
+                    out=acc_y[:],
+                    lhsT=w2_codes[d // 4][:, cols].bitcast(FP8X4),
+                    lhsT_scale=w2_scales[d // 4][:, cols],
+                    rhs=hc[:].bitcast(FP8X4),
+                    rhs_scale=hs[:],
+                    start=True,
+                    stop=True,
+                )
+            if i < E:
+                wi_b0 = interleave(raws[2], "S", order, "tc", "b%d0" % e)
+                st["cb0"] = quantise(wi_b0, "b%d0" % e)
+                ga = small.tile([P, PACK * C], F32, tag="ga", name="ga%d" % e)
+                nc.scalar.activation(
+                    ga[:].rearrange("p (c t) -> p c t", t=4), acc_a[:].rearrange("p t c -> p c t"), GELU
+                )
+                st["ga"] = ga
+            if i > 0:
+                yg = order.tile([P, C], F32, tag="tc", name="yg%d" % d, align_bytes=64)
+                nc.vector.tensor_tensor(out=yg[:], in0=acc_y[:], in1=gate_sb[:, d * C : (d + 1) * C], op=MULT)
+                nc.vector.tensor_copy(
+                    out=window[:].indirect(offsets[:, d * C // 16 : (d + 1) * C // 16]), in_=yg[:]
+                )
+            if i < E:
+                st["wi_b1"] = interleave(raws[3], "V" if e == E - 1 else "S", grouped, "wi", "b%d1" % e)
+
+        nc.sync.dma_start(out, window[:])

@@ -26,7 +26,8 @@ def tile_routed_moe_kernel(tc, xT, w1, w3, w2, gate, offs, out):
     nc = tc.nc
     with ExitStack() as ctx:
         held = ctx.enter_context(tc.tile_pool(name="held", bufs=1))
-        stream = ctx.enter_context(tc.tile_pool(name="stream", bufs=8))
+        stream = ctx.enter_context(tc.tile_pool(name="stream", bufs=6))
+        turn = ctx.enter_context(tc.tile_pool(name="turn", bufs=1))
         grouped = ctx.enter_context(tc.tile_pool(name="grouped", bufs=2))
         quant = ctx.enter_context(tc.tile_pool(name="quant", bufs=10))
         small = ctx.enter_context(tc.tile_pool(name="small", bufs=2))
@@ -106,8 +107,8 @@ def tile_routed_moe_kernel(tc, xT, w1, w3, w2, gate, offs, out):
 
         window = held.tile([P, T], F32, name="window")
 
-        def load_chunk(w, e, g, label):
-            raw = stream.tile([P, CHUNK], F32, tag="raw", name="raw_%s" % label)
+        def load_chunk(w, e, g, label, pool=stream, tag="raw"):
+            raw = pool.tile([P, CHUNK], F32, tag=tag, name="raw_%s" % label)
             nc.sync.dma_start(raw[:], w[e].rearrange("(g p j) c -> g p (j c)", p=P, j=PACK)[g])
             return raw
 
@@ -151,7 +152,7 @@ def tile_routed_moe_kernel(tc, xT, w1, w3, w2, gate, offs, out):
                     load_chunk(w1, e, 0, "a%d0" % e),
                     load_chunk(w1, e, 1, "a%d1" % e),
                     load_chunk(w3, e, 0, "b%d0" % e),
-                    load_chunk(w3, e, 1, "b%d1" % e),
+                    load_chunk(w3, e, 1, "b%d1" % e, turn, "rb%d" % (e % 2)),
                 ]
                 wi_a0 = interleave(raws[0], "V", order, "ta", "a%d0" % e)
             if i > 0:
@@ -191,11 +192,6 @@ def tile_routed_moe_kernel(tc, xT, w1, w3, w2, gate, offs, out):
             if i < E:
                 wi_b0 = interleave(raws[2], "S", order, "tc", "b%d0" % e)
                 st["cb0"] = quantise(wi_b0, "b%d0" % e)
-                ga = small.tile([P, PACK * C], F32, tag="ga", name="ga%d" % e)
-                nc.scalar.activation(
-                    ga[:].rearrange("p (c t) -> p c t", t=4), acc_a[:].rearrange("p t c -> p c t"), GELU
-                )
-                st["ga"] = ga
             if i > 0:
                 yg = order.tile([P, C], F32, tag="tc", name="yg%d" % d, align_bytes=64)
                 nc.vector.tensor_tensor(out=yg[:], in0=acc_y[:], in1=gate_sb[:, d * C : (d + 1) * C], op=MULT)
@@ -204,5 +200,13 @@ def tile_routed_moe_kernel(tc, xT, w1, w3, w2, gate, offs, out):
                 )
             if i < E:
                 st["wi_b1"] = interleave(raws[3], "V" if e == E - 1 else "S", grouped, "wi", "b%d1" % e)
+                if e < E - 1:
+                    ga = turn.tile([P, PACK * C], F32, tag="rb%d" % (e % 2), name="ga%d" % e)
+                else:
+                    ga = small.tile([P, PACK * C], F32, tag="ga", name="ga%d" % e)
+                nc.scalar.activation(
+                    ga[:].rearrange("p (c t) -> p c t", t=4), acc_a[:].rearrange("p t c -> p c t"), GELU
+                )
+                st["ga"] = ga
 
         nc.sync.dma_start(out, window[:])

@@ -20,6 +20,7 @@ K_PASS = P * PACK
 PASSES = K // K_PASS
 CHUNK = 2048
 HALF = 512
+SHARE = 64
 
 
 def tile_routed_moe_kernel(tc, xT, w1, w3, w2, gate, offs, out):
@@ -114,11 +115,13 @@ def tile_routed_moe_kernel(tc, xT, w1, w3, w2, gate, offs, out):
 
         def interleave(raw, engine, pool, tag, label):
             wi = pool.tile([P, CHUNK], BF16, tag=tag, name="wi_%s" % label, align_bytes=64)
-            copy_on(
-                engine,
-                wi[:].rearrange("p (t m j) -> p m j t", t=4, j=PACK),
-                raw[:].rearrange("p (j m t) -> p m j t", t=4, j=PACK),
-            )
+            dst = wi[:].rearrange("p (t m j) -> p m j t", t=4, j=PACK)
+            src = raw[:].rearrange("p (j m t) -> p m j t", t=4, j=PACK)
+            if engine == "VS":
+                copy_on("V", dst[:, 0:SHARE], src[:, 0:SHARE])
+                copy_on("S", dst[:, SHARE:P], src[:, SHARE:P])
+            else:
+                copy_on(engine, dst, src)
             return wi
 
         def quantise(wi, label):
@@ -190,7 +193,7 @@ def tile_routed_moe_kernel(tc, xT, w1, w3, w2, gate, offs, out):
                     stop=True,
                 )
             if i < E:
-                wi_b0 = interleave(raws[2], "S", order, "tc", "b%d0" % e)
+                wi_b0 = interleave(raws[2], "VS" if e < E - 1 else "S", order, "tc", "b%d0" % e)
                 st["cb0"] = quantise(wi_b0, "b%d0" % e)
             if i > 0:
                 yg = order.tile([P, C], F32, tag="tc", name="yg%d" % d, align_bytes=64)

@@ -21,6 +21,7 @@ PASSES = K // K_PASS
 CHUNK = 2048
 HALF = 512
 SHARE = 64
+SHARE_LAST = 84
 
 
 def tile_routed_moe_kernel(tc, xT, w1, w3, w2, gate, offs, out):
@@ -113,13 +114,13 @@ def tile_routed_moe_kernel(tc, xT, w1, w3, w2, gate, offs, out):
             nc.sync.dma_start(raw[:], w[e].rearrange("(g p j) c -> g p (j c)", p=P, j=PACK)[g])
             return raw
 
-        def interleave(raw, engine, pool, tag, label):
+        def interleave(raw, engine, pool, tag, label, share=SHARE):
             wi = pool.tile([P, CHUNK], BF16, tag=tag, name="wi_%s" % label, align_bytes=64)
             dst = wi[:].rearrange("p (t m j) -> p m j t", t=4, j=PACK)
             src = raw[:].rearrange("p (j m t) -> p m j t", t=4, j=PACK)
             if engine == "VS":
-                copy_on("V", dst[:, 0:SHARE], src[:, 0:SHARE])
-                copy_on("S", dst[:, SHARE:P], src[:, SHARE:P])
+                copy_on("V", dst[:, 0:share], src[:, 0:share])
+                copy_on("S", dst[:, share:P], src[:, share:P])
             else:
                 copy_on(engine, dst, src)
             return wi
@@ -146,7 +147,13 @@ def tile_routed_moe_kernel(tc, xT, w1, w3, w2, gate, offs, out):
                         stop=(g == PASSES - 1),
                     )
 
+        def way_back(acc, d, tag):
+            yg = order.tile([P, C], F32, tag=tag, name="yg%d" % d, align_bytes=64)
+            nc.vector.tensor_tensor(out=yg[:], in0=acc[:], in1=gate_sb[:, d * C : (d + 1) * C], op=MULT)
+            nc.vector.tensor_copy(out=window[:].indirect(offsets[:, d * C // 16 : (d + 1) * C // 16]), in_=yg[:])
+
         st = {}
+        acc_y = None
         for i in range(E + 1):
             e = i
             d = i - 1
@@ -162,6 +169,8 @@ def tile_routed_moe_kernel(tc, xT, w1, w3, w2, gate, offs, out):
                 cb1 = quantise(st["wi_b1"], "b%d1" % d)
                 acc_b = psum.tile([P, 4, C], F32, tag="acc_b", name="acc_b%d" % d)
                 first_layer(acc_b, [st["cb0"], cb1], d)
+            if i == E:
+                way_back(acc_y, d - 1, "tl")
             if i < E:
                 ca0 = quantise(wi_a0, "a%d0" % e)
             if i > 0:
@@ -193,20 +202,16 @@ def tile_routed_moe_kernel(tc, xT, w1, w3, w2, gate, offs, out):
                     stop=True,
                 )
             if i < E:
-                wi_b0 = interleave(raws[2], "VS" if e < E - 1 else "S", order, "tc", "b%d0" % e)
+                wi_b0 = interleave(raws[2], "VS", order, "tc", "b%d0" % e)
                 st["cb0"] = quantise(wi_b0, "b%d0" % e)
-            if i > 0:
-                yg = order.tile([P, C], F32, tag="tc", name="yg%d" % d, align_bytes=64)
-                nc.vector.tensor_tensor(out=yg[:], in0=acc_y[:], in1=gate_sb[:, d * C : (d + 1) * C], op=MULT)
-                nc.vector.tensor_copy(
-                    out=window[:].indirect(offsets[:, d * C // 16 : (d + 1) * C // 16]), in_=yg[:]
-                )
+            if i > 0 and i != E - 1:
+                way_back(acc_y, d, "tc")
             if i < E:
-                st["wi_b1"] = interleave(raws[3], "V" if e == E - 1 else "S", grouped, "wi", "b%d1" % e)
                 if e < E - 1:
-                    ga = turn.tile([P, PACK * C], F32, tag="rb%d" % (e % 2), name="ga%d" % e)
+                    st["wi_b1"] = interleave(raws[3], "S", grouped, "wi", "b%d1" % e)
                 else:
-                    ga = small.tile([P, PACK * C], F32, tag="ga", name="ga%d" % e)
+                    st["wi_b1"] = interleave(raws[3], "VS", order, "tl", "b%d1" % e, SHARE_LAST)
+                ga = turn.tile([P, PACK * C], F32, tag="rb%d" % (e % 2), name="ga%d" % e)
                 nc.scalar.activation(
                     ga[:].rearrange("p (c t) -> p c t", t=4), acc_a[:].rearrange("p t c -> p c t"), GELU
                 )

@@ -20,6 +20,8 @@ K_PASS = P * PACK
 PASSES = K // K_PASS
 CHUNK = 2048
 HALF = 512
+W2_EARLY = ((0, 4), (4, 2), (6, 1))
+GATE_EARLY = 6
 SHARE = 64
 SHARE_LAST = 84
 
@@ -64,8 +66,9 @@ def tile_routed_moe_kernel(tc, xT, w1, w3, w2, gate, offs, out):
                 )
                 pairs[(g, u)] = pair
 
-        gate_sb = held.tile([P, E * C], F32, name="gate_sb")
-        nc.sync.dma_start(gate_sb[:], gate)
+        gate_early = held.tile([P, GATE_EARLY * C], F32, name="gate_early")
+        nc.sync.dma_start(gate_early[:], gate[:, 0 : GATE_EARLY * C])
+        gate_late = held.tile([P, (E - GATE_EARLY) * C], F32, name="gate_late")
 
         x_codes = []
         x_scales = []
@@ -90,22 +93,28 @@ def tile_routed_moe_kernel(tc, xT, w1, w3, w2, gate, offs, out):
             x_scales.append(xs)
 
         w2_rows = w2.rearrange("e (p j) n -> p e (j n)", p=P, j=PACK)
-        w2_codes = []
-        w2_scales = []
-        for half in range(2):
-            raw = stream.tile([P, CHUNK], F32, tag="raw", name="w2raw%d" % half)
-            nc.sync.dma_start(raw[:].rearrange("p (e f) -> p e f", e=4), w2_rows[:, 4 * half : 4 * half + 4, :])
-            wi = grouped.tile([P, CHUNK], BF16, tag="wi", name="w2i%d" % half, align_bytes=64)
+        w2_of = {}
+
+        def load_w2(first, count):
+            raw = stream.tile([P, count * PACK * N], F32, tag="raw", name="w2raw%d" % first)
+            nc.sync.dma_start(raw[:].rearrange("p (e f) -> p e f", e=count), w2_rows[:, first : first + count, :])
+            return raw
+
+        def prepare_w2(raw, first, count):
+            wi = grouped.tile([P, count * PACK * N], BF16, tag="wi", name="w2i%d" % first, align_bytes=64)
             copy_on(
                 "S",
-                wi[:].rearrange("p (e c i j) -> p e c j i", e=4, i=4, j=PACK),
-                raw[:].rearrange("p (e j c i) -> p e c j i", e=4, i=4, j=PACK),
+                wi[:].rearrange("p (e c i j) -> p e c j i", e=count, i=4, j=PACK),
+                raw[:].rearrange("p (e j c i) -> p e c j i", e=count, i=4, j=PACK),
             )
-            wc = held.tile([P, CHUNK // PACK], U32, name="w2c%d" % half, align_bytes=64)
-            ws = held.tile([P, CHUNK // PACK], U8, name="w2s%d" % half, align_bytes=64)
+            wc = held.tile([P, count * N], U32, name="w2c%d" % first, align_bytes=64)
+            ws = held.tile([P, count * N], U8, name="w2s%d" % first, align_bytes=64)
             nc.vector.quantize_mx(out=wc[:].bitcast(FP8X4), scales=ws[:], in_=wi[:])
-            w2_codes.append(wc)
-            w2_scales.append(ws)
+            for k in range(count):
+                w2_of[first + k] = (wc, ws, slice(k * N, (k + 1) * N))
+
+        for first, count in W2_EARLY:
+            prepare_w2(load_w2(first, count), first, count)
 
         window = held.tile([P, T], F32, name="window")
 
@@ -149,11 +158,16 @@ def tile_routed_moe_kernel(tc, xT, w1, w3, w2, gate, offs, out):
 
         def way_back(acc, d, tag):
             yg = order.tile([P, C], F32, tag=tag, name="yg%d" % d, align_bytes=64)
-            nc.vector.tensor_tensor(out=yg[:], in0=acc[:], in1=gate_sb[:, d * C : (d + 1) * C], op=MULT)
+            if d < GATE_EARLY:
+                weight = gate_early[:, d * C : (d + 1) * C]
+            else:
+                weight = gate_late[:, (d - GATE_EARLY) * C : (d - GATE_EARLY + 1) * C]
+            nc.vector.tensor_tensor(out=yg[:], in0=acc[:], in1=weight, op=MULT)
             nc.vector.tensor_copy(out=window[:].indirect(offsets[:, d * C // 16 : (d + 1) * C // 16]), in_=yg[:])
 
         st = {}
         acc_y = None
+        w2_last = None
         for i in range(E + 1):
             e = i
             d = i - 1
@@ -164,12 +178,16 @@ def tile_routed_moe_kernel(tc, xT, w1, w3, w2, gate, offs, out):
                     load_chunk(w3, e, 0, "b%d0" % e),
                     load_chunk(w3, e, 1, "b%d1" % e, turn, "rb%d" % (e % 2)),
                 ]
+                if e == E - 1:
+                    w2_last = load_w2(e, 1)
+                    nc.sync.dma_start(gate_late[:], gate[:, GATE_EARLY * C : E * C])
                 wi_a0 = interleave(raws[0], "V", order, "ta", "a%d0" % e)
             if i > 0:
                 cb1 = quantise(st["wi_b1"], "b%d1" % d)
                 acc_b = psum.tile([P, 4, C], F32, tag="acc_b", name="acc_b%d" % d)
                 first_layer(acc_b, [st["cb0"], cb1], d)
             if i == E:
+                prepare_w2(w2_last, d, 1)
                 way_back(acc_y, d - 1, "tl")
             if i < E:
                 ca0 = quantise(wi_a0, "a%d0" % e)
@@ -191,11 +209,11 @@ def tile_routed_moe_kernel(tc, xT, w1, w3, w2, gate, offs, out):
                 hs = small.tile([P, C], U8, tag="hs", name="hs%d" % d, align_bytes=64)
                 nc.vector.quantize_mx(out=hc[:].bitcast(FP8X4), scales=hs[:], in_=hq[:])
                 acc_y = psum.tile([P, C], F32, tag="acc_y", name="acc_y%d" % d)
-                cols = slice((d % 4) * N, (d % 4 + 1) * N)
+                wc2, ws2, cols = w2_of[d]
                 nc.tensor.matmul_mx(
                     out=acc_y[:],
-                    lhsT=w2_codes[d // 4][:, cols].bitcast(FP8X4),
-                    lhsT_scale=w2_scales[d // 4][:, cols],
+                    lhsT=wc2[:, cols].bitcast(FP8X4),
+                    lhsT_scale=ws2[:, cols],
                     rhs=hc[:].bitcast(FP8X4),
                     rhs_scale=hs[:],
                     start=True,

@@ -19,6 +19,7 @@ PACK = 4
 K_PASS = P * PACK
 PASSES = K // K_PASS
 CHUNK = 2048
+RAW_ALIGN = 8192
 HALF = 512
 W2_EARLY = ((0, 4), (4, 2), (6, 1))
 GATE_EARLY = 6
@@ -56,7 +57,7 @@ def tile_routed_moe_kernel(tc, xT, w1, w3, w2, gate, offs, out):
         pairs = {}
         for g in range(PASSES):
             for u in range(2):
-                raw = stream.tile([P, CHUNK], F32, tag="raw", name="xraw%d%d" % (g, u))
+                raw = stream.tile([P, CHUNK], F32, tag="raw", name="xraw%d%d" % (g, u), align_bytes=RAW_ALIGN)
                 nc.sync.dma_start(raw[:], x_planes[g, u])
                 pair = held.tile([P, 2 * T], BF16, name="pair%d%d" % (g, u))
                 copy_on(
@@ -96,7 +97,7 @@ def tile_routed_moe_kernel(tc, xT, w1, w3, w2, gate, offs, out):
         w2_of = {}
 
         def load_w2(first, count):
-            raw = stream.tile([P, count * PACK * N], F32, tag="raw", name="w2raw%d" % first)
+            raw = stream.tile([P, count * PACK * N], F32, tag="raw", name="w2raw%d" % first, align_bytes=RAW_ALIGN)
             nc.sync.dma_start(raw[:].rearrange("p (e f) -> p e f", e=count), w2_rows[:, first : first + count, :])
             return raw
 
@@ -119,7 +120,7 @@ def tile_routed_moe_kernel(tc, xT, w1, w3, w2, gate, offs, out):
         window = held.tile([P, T], F32, name="window")
 
         def load_chunk(w, e, g, label, pool=stream, tag="raw"):
-            raw = pool.tile([P, CHUNK], F32, tag=tag, name="raw_%s" % label)
+            raw = pool.tile([P, CHUNK], F32, tag=tag, name="raw_%s" % label, align_bytes=RAW_ALIGN)
             nc.sync.dma_start(raw[:], w[e].rearrange("(g p j) c -> g p (j c)", p=P, j=PACK)[g])
             return raw
 
@@ -229,7 +230,7 @@ def tile_routed_moe_kernel(tc, xT, w1, w3, w2, gate, offs, out):
                     st["wi_b1"] = interleave(raws[3], "S", grouped, "wi", "b%d1" % e)
                 else:
                     st["wi_b1"] = interleave(raws[3], "VS", order, "tl", "b%d1" % e, SHARE_LAST)
-                ga = turn.tile([P, PACK * C], F32, tag="rb%d" % (e % 2), name="ga%d" % e)
+                ga = turn.tile([P, PACK * C], F32, tag="rb%d" % (e % 2), name="ga%d" % e, align_bytes=RAW_ALIGN)
                 nc.scalar.activation(
                     ga[:].rearrange("p (c t) -> p c t", t=4), acc_a[:].rearrange("p t c -> p c t"), GELU
                 )

@@ -135,10 +135,16 @@ def tile_routed_moe_kernel(tc, xT, w1, w3, w2, gate, offs, out):
                 copy_on(engine, dst, src)
             return wi
 
-        def quantise(wi, label):
+        def quantise(wi, label, pieces=1):
             wc = quant.tile([P, H], U32, tag="wc", name="wc_%s" % label, align_bytes=64)
             ws = quant.tile([P, H], U8, tag="ws", name="ws_%s" % label, align_bytes=64)
-            nc.vector.quantize_mx(out=wc[:].bitcast(FP8X4), scales=ws[:], in_=wi[:])
+            width = H // pieces
+            for q in range(pieces):
+                nc.vector.quantize_mx(
+                    out=wc[:, q * width : (q + 1) * width].bitcast(FP8X4),
+                    scales=ws[:, q * width : (q + 1) * width],
+                    in_=wi[:, q * width * PACK : (q + 1) * width * PACK],
+                )
             return wc, ws
 
         def first_layer(acc, codes, e):
@@ -166,6 +172,16 @@ def tile_routed_moe_kernel(tc, xT, w1, w3, w2, gate, offs, out):
             nc.vector.tensor_tensor(out=yg[:], in0=acc[:], in1=weight, op=MULT)
             nc.vector.tensor_copy(out=window[:].indirect(offsets[:, d * C // 16 : (d + 1) * C // 16]), in_=yg[:])
 
+        def late_way_back(acc, d, pool, tag, align):
+            ys = pool.tile([P, C], F32, tag=tag, name="ys%d" % d, align_bytes=align)
+            nc.scalar.copy(out=ys[:], in_=acc[:])
+            nc.vector.tensor_tensor(
+                out=window[:].indirect(offsets[:, d * C // 16 : (d + 1) * C // 16]),
+                in0=ys[:],
+                in1=gate_late[:, (d - GATE_EARLY) * C : (d - GATE_EARLY + 1) * C],
+                op=MULT,
+            )
+
         st = {}
         acc_y = None
         w2_last = None
@@ -184,12 +200,12 @@ def tile_routed_moe_kernel(tc, xT, w1, w3, w2, gate, offs, out):
                     nc.sync.dma_start(gate_late[:], gate[:, GATE_EARLY * C : E * C])
                 wi_a0 = interleave(raws[0], "V", order, "ta", "a%d0" % e)
             if i > 0:
-                cb1 = quantise(st["wi_b1"], "b%d1" % d)
+                cb1 = quantise(st["wi_b1"], "b%d1" % d, 1 if d < E - 1 else 2)
                 acc_b = psum.tile([P, 4, C], F32, tag="acc_b", name="acc_b%d" % d)
                 first_layer(acc_b, [st["cb0"], cb1], d)
             if i == E:
                 prepare_w2(w2_last, d, 1)
-                way_back(acc_y, d - 1, "tl")
+                acc_y_held = acc_y
             if i < E:
                 ca0 = quantise(wi_a0, "a%d0" % e)
             if i > 0:
@@ -223,8 +239,11 @@ def tile_routed_moe_kernel(tc, xT, w1, w3, w2, gate, offs, out):
             if i < E:
                 wi_b0 = interleave(raws[2], "VS", order, "tc", "b%d0" % e)
                 st["cb0"] = quantise(wi_b0, "b%d0" % e)
-            if i > 0 and i != E - 1:
+            if 0 < i < E - 1:
                 way_back(acc_y, d, "tc")
+            if i == E:
+                late_way_back(acc_y_held, d - 1, turn, "rb%d" % (d % 2), RAW_ALIGN)
+                late_way_back(acc_y, d, order, "tc", 64)
             if i < E:
                 if e < E - 1:
                     st["wi_b1"] = interleave(raws[3], "S", grouped, "wi", "b%d1" % e)

@@ -200,7 +200,7 @@ def tile_routed_moe_kernel(tc, xT, w1, w3, w2, gate, offs, out):
                     nc.sync.dma_start(gate_late[:], gate[:, GATE_EARLY * C : E * C])
                 wi_a0 = interleave(raws[0], "V", order, "ta", "a%d0" % e)
             if i > 0:
-                cb1 = quantise(st["wi_b1"], "b%d1" % d, 1 if d < E - 1 else 2)
+                cb1 = quantise(st["wi_b1"], "b%d1" % d, 1 if d < E - 1 else 4)
                 acc_b = psum.tile([P, 4, C], F32, tag="acc_b", name="acc_b%d" % d)
                 first_layer(acc_b, [st["cb0"], cb1], d)
             if i == E:

from contextlib import ExitStack

import concourse.mybir as mybir

K, T, E, C, H, N = 1024, 1024, 8, 128, 512, 128
FLOPS = 2 * E * C * (2 * K * H + H * N)

F32 = mybir.dt.float32
BF16 = mybir.dt.bfloat16
U32 = mybir.dt.uint32
U16 = mybir.dt.uint16
U8 = mybir.dt.uint8
FP8X4 = mybir.dt.float8_e4m3fn_x4
GELU = mybir.ActivationFunctionType.Gelu_apprx_tanh
MULT = mybir.AluOpType.mult

P = 128
PACK = 4
K_PASS = P * PACK
PASSES = K // K_PASS
CHUNK = 2048
RAW_ALIGN = 8192
HALF = 512
W2_EARLY = ((0, 4), (4, 2), (6, 1))
GATE_EARLY = 6
SHARE = 64
SHARE_LAST = 84


def tile_routed_moe_kernel(tc, xT, w1, w3, w2, gate, offs, out):
    nc = tc.nc
    with ExitStack() as ctx:
        held = ctx.enter_context(tc.tile_pool(name="held", bufs=1))
        stream = ctx.enter_context(tc.tile_pool(name="stream", bufs=6))
        turn = ctx.enter_context(tc.tile_pool(name="turn", bufs=1))
        grouped = ctx.enter_context(tc.tile_pool(name="grouped", bufs=2))
        quant = ctx.enter_context(tc.tile_pool(name="quant", bufs=10))
        small = ctx.enter_context(tc.tile_pool(name="small", bufs=2))
        order = ctx.enter_context(tc.tile_pool(name="order", bufs=1))
        psum = ctx.enter_context(tc.psum_pool(name="psum", bufs=2))

        offsets = held.tile([P, E * C // 16], U16, name="offsets")
        nc.sync.dma_start(offsets[:], offs)

        warm_in = held.tile([P, 1], F32, name="warm_in")
        warm_out = held.tile([P, 1], F32, name="warm_out")
        nc.vector.memset(warm_in[:], 0.0)
        nc.scalar.activation(warm_out[:], warm_in[:], GELU)

        def copy_on(engine, dst, src):
            if engine == "V":
                nc.vector.tensor_copy(out=dst, in_=src)
            else:
                nc.scalar.copy(out=dst, in_=src)

        x_planes = xT.rearrange("(g p u e) n -> g u p (e n)", p=P, u=2, e=2)
        pairs = {}
        for g in range(PASSES):
            for u in range(2):
                raw = stream.tile([P, CHUNK], F32, tag="raw", name="xraw%d%d" % (g, u), align_bytes=RAW_ALIGN)
                nc.sync.dma_start(raw[:], x_planes[g, u])
                pair = held.tile([P, 2 * T], BF16, name="pair%d%d" % (g, u))
                copy_on(
                    "S",
                    pair[:].rearrange("p (n e) -> p n e", e=2),
                    raw[:].rearrange("p (e n) -> p n e", e=2),
                )
                pairs[(g, u)] = pair

        gate_early = held.tile([P, GATE_EARLY * C], F32, name="gate_early")
        nc.sync.dma_start(gate_early[:], gate[:, 0 : GATE_EARLY * C])
        gate_late = held.tile([P, (E - GATE_EARLY) * C], F32, name="gate_late")

        x_codes = []
        x_scales = []
        for g in range(PASSES):
            xg = held.tile([P, PACK * E * C], BF16, name="xg%d" % g, align_bytes=64)
            xg_words = xg[:].bitcast(U32).rearrange("p (s u) -> p s u", u=2)
            for u in range(2):
                for h in range(E * C // HALF):
                    nc.vector.tensor_copy(
                        out=xg_words[:, h * HALF : (h + 1) * HALF, u],
                        in_=pairs[(g, u)][:].bitcast(U32).indirect(offsets[:, h * HALF // 16 : (h + 1) * HALF // 16]),
                    )
            xc = held.tile([P, E * C], U32, name="xc%d" % g, align_bytes=64)
            xs = held.tile([P, E * C], U8, name="xs%d" % g, align_bytes=64)
            for h in range(E * C // HALF):
                nc.vector.quantize_mx(
                    out=xc[:, h * HALF : (h + 1) * HALF].bitcast(FP8X4),
                    scales=xs[:, h * HALF : (h + 1) * HALF],
                    in_=xg[:, h * HALF * PACK : (h + 1) * HALF * PACK],
                )
            x_codes.append(xc)
            x_scales.append(xs)

        w2_rows = w2.rearrange("e (p j) n -> p e (j n)", p=P, j=PACK)
        w2_of = {}

        def load_w2(first, count):
            raw = stream.tile([P, count * PACK * N], F32, tag="raw", name="w2raw%d" % first, align_bytes=RAW_ALIGN)
            nc.sync.dma_start(raw[:].rearrange("p (e f) -> p e f", e=count), w2_rows[:, first : first + count, :])
            return raw

        def prepare_w2(raw, first, count):
            wi = grouped.tile([P, count * PACK * N], BF16, tag="wi", name="w2i%d" % first, align_bytes=64)
            copy_on(
                "S",
                wi[:].rearrange("p (e c i j) -> p e c j i", e=count, i=4, j=PACK),
                raw[:].rearrange("p (e j c i) -> p e c j i", e=count, i=4, j=PACK),
            )
            wc = held.tile([P, count * N], U32, name="w2c%d" % first, align_bytes=64)
            ws = held.tile([P, count * N], U8, name="w2s%d" % first, align_bytes=64)
            nc.vector.quantize_mx(out=wc[:].bitcast(FP8X4), scales=ws[:], in_=wi[:])
            for k in range(count):
                w2_of[first + k] = (wc, ws, slice(k * N, (k + 1) * N))

        for first, count in W2_EARLY:
            prepare_w2(load_w2(first, count), first, count)

        window = held.tile([P, T], F32, name="window")

        def load_chunk(w, e, g, label, pool=stream, tag="raw"):
            raw = pool.tile([P, CHUNK], F32, tag=tag, name="raw_%s" % label, align_bytes=RAW_ALIGN)
            nc.sync.dma_start(raw[:], w[e].rearrange("(g p j) c -> g p (j c)", p=P, j=PACK)[g])
            return raw

        def interleave(raw, engine, pool, tag, label, share=SHARE):
            wi = pool.tile([P, CHUNK], BF16, tag=tag, name="wi_%s" % label, align_bytes=64)
            dst = wi[:].rearrange("p (t m j) -> p m j t", t=4, j=PACK)
            src = raw[:].rearrange("p (j m t) -> p m j t", t=4, j=PACK)
            if engine == "VS":
                copy_on("V", dst[:, 0:share], src[:, 0:share])
                copy_on("S", dst[:, share:P], src[:, share:P])
            else:
                copy_on(engine, dst, src)
            return wi

        def quantise(wi, label, pieces=1):
            wc = quant.tile([P, H], U32, tag="wc", name="wc_%s" % label, align_bytes=64)
            ws = quant.tile([P, H], U8, tag="ws", name="ws_%s" % label, align_bytes=64)
            width = H // pieces
            for q in range(pieces):
                nc.vector.quantize_mx(
                    out=wc[:, q * width : (q + 1) * width].bitcast(FP8X4),
                    scales=ws[:, q * width : (q + 1) * width],
                    in_=wi[:, q * width * PACK : (q + 1) * width * PACK],
                )
            return wc, ws

        def first_layer(acc, codes, e):
            slots = slice(e * C, (e + 1) * C)
            for t in range(4):
                cols = slice(t * P, (t + 1) * P)
                for g in range(PASSES):
                    wc, ws = codes[g]
                    nc.tensor.matmul_mx(
                        out=acc[:, t, :],
                        lhsT=wc[:, cols].bitcast(FP8X4),
                        lhsT_scale=ws[:, cols],
                        rhs=x_codes[g][:, slots].bitcast(FP8X4),
                        rhs_scale=x_scales[g][:, slots],
                        start=(g == 0),
                        stop=(g == PASSES - 1),
                    )

        def way_back(acc, d, tag):
            yg = order.tile([P, C], F32, tag=tag, name="yg%d" % d, align_bytes=64)
            if d < GATE_EARLY:
                weight = gate_early[:, d * C : (d + 1) * C]
            else:
                weight = gate_late[:, (d - GATE_EARLY) * C : (d - GATE_EARLY + 1) * C]
            nc.vector.tensor_tensor(out=yg[:], in0=acc[:], in1=weight, op=MULT)
            nc.vector.tensor_copy(out=window[:].indirect(offsets[:, d * C // 16 : (d + 1) * C // 16]), in_=yg[:])

        def late_way_back(acc, d, pool, tag, align):
            ys = pool.tile([P, C], F32, tag=tag, name="ys%d" % d, align_bytes=align)
            nc.scalar.copy(out=ys[:], in_=acc[:])
            nc.vector.tensor_tensor(
                out=window[:].indirect(offsets[:, d * C // 16 : (d + 1) * C // 16]),
                in0=ys[:],
                in1=gate_late[:, (d - GATE_EARLY) * C : (d - GATE_EARLY + 1) * C],
                op=MULT,
            )

        st = {}
        acc_y = None
        w2_last = None
        for i in range(E + 1):
            e = i
            d = i - 1
            if i < E:
                raws = [
                    load_chunk(w1, e, 0, "a%d0" % e),
                    load_chunk(w1, e, 1, "a%d1" % e),
                    load_chunk(w3, e, 0, "b%d0" % e),
                    load_chunk(w3, e, 1, "b%d1" % e, turn, "rb%d" % (e % 2)),
                ]
                if e == E - 1:
                    w2_last = load_w2(e, 1)
                    nc.sync.dma_start(gate_late[:], gate[:, GATE_EARLY * C : E * C])
                wi_a0 = interleave(raws[0], "V", order, "ta", "a%d0" % e)
            if i > 0:
                cb1 = quantise(st["wi_b1"], "b%d1" % d, 1 if d < E - 1 else 4)
                acc_b = psum.tile([P, 4, C], F32, tag="acc_b", name="acc_b%d" % d)
                first_layer(acc_b, [st["cb0"], cb1], d)
            if i == E:
                prepare_w2(w2_last, d, 1)
                acc_y_held = acc_y
            if i < E:
                ca0 = quantise(wi_a0, "a%d0" % e)
            if i > 0:
                hq = order.tile([P, PACK * C], BF16, tag="ta", name="hq%d" % d, align_bytes=64)
                nc.vector.tensor_tensor(
                    out=hq[:].rearrange("p (c t) -> p c t", t=4),
                    in0=acc_b[:].rearrange("p t c -> p c t"),
                    in1=st["ga"][:].rearrange("p (c t) -> p c t", t=4),
                    op=MULT,
                )
            if i < E:
                wi_a1 = interleave(raws[1], "S", order, "tb", "a%d1" % e)
                ca1 = quantise(wi_a1, "a%d1" % e)
                acc_a = psum.tile([P, 4, C], F32, tag="acc_a", name="acc_a%d" % e)
                first_layer(acc_a, [ca0, ca1], e)
            if i > 0:
                hc = order.tile([P, C], U32, tag="tb", name="hc%d" % d, align_bytes=64)
                hs = small.tile([P, C], U8, tag="hs", name="hs%d" % d, align_bytes=64)
                nc.vector.quantize_mx(out=hc[:].bitcast(FP8X4), scales=hs[:], in_=hq[:])
                acc_y = psum.tile([P, C], F32, tag="acc_y", name="acc_y%d" % d)
                wc2, ws2, cols = w2_of[d]
                nc.tensor.matmul_mx(
                    out=acc_y[:],
                    lhsT=wc2[:, cols].bitcast(FP8X4),
                    lhsT_scale=ws2[:, cols],
                    rhs=hc[:].bitcast(FP8X4),
                    rhs_scale=hs[:],
                    start=True,
                    stop=True,
                )
            if i < E:
                wi_b0 = interleave(raws[2], "VS", order, "tc", "b%d0" % e)
                st["cb0"] = quantise(wi_b0, "b%d0" % e)
            if 0 < i < E - 1:
                way_back(acc_y, d, "tc")
            if i == E:
                late_way_back(acc_y_held, d - 1, turn, "rb%d" % (d % 2), RAW_ALIGN)
                late_way_back(acc_y, d, order, "tc", 64)
            if i < E:
                if e < E - 1:
                    st["wi_b1"] = interleave(raws[3], "S", grouped, "wi", "b%d1" % e)
                else:
                    st["wi_b1"] = interleave(raws[3], "VS", order, "tl", "b%d1" % e, SHARE_LAST)
                ga = turn.tile([P, PACK * C], F32, tag="rb%d" % (e % 2), name="ga%d" % e, align_bytes=RAW_ALIGN)
                nc.scalar.activation(
                    ga[:].rearrange("p (c t) -> p c t", t=4), acc_a[:].rearrange("p t c -> p c t"), GELU
                )
                st["ga"] = ga

        nc.sync.dma_start(out, window[:])
